import numpy as np
import ml_dtypes


def mxq(x, axis, fmt="e4m3"):
    dtype, down = {"e4m3": (ml_dtypes.float8_e4m3fn, 7), "e5m2": (ml_dtypes.float8_e5m2, 14)}[fmt]
    v = np.moveaxis(np.asarray(x, np.float32).astype(ml_dtypes.bfloat16).astype(np.float64), axis, -1)
    blocks = v.reshape(v.shape[:-1] + (-1, 32))
    amax = np.abs(blocks).max(-1, keepdims=True)
    byte = np.maximum(np.where(amax > 0, np.frexp(amax)[1] - 1 + 127, 0) - down, 1)
    scale = np.exp2(byte - 127.0)
    codes = (blocks / scale).astype(np.float32).astype(dtype).astype(np.float64)
    return np.moveaxis((codes * scale).reshape(v.shape), -1, axis)


WIDE = False


def mx_kscale(k):
    if not WIDE:
        return np.ones(k)
    levels = np.array([10, -10, 5, -5, 0])
    if k % 512:
        return np.exp2(np.random.permutation(np.resize(levels, k // 32))).repeat(32)
    a = np.empty((k // 512, 16))
    for p in range(k // 512):
        a[p, :8] = np.random.permutation(np.resize(levels, 8))
        for g in range(8):
            far = levels[np.abs(levels - a[p, g]) >= 10]
            a[p, g + 8] = far[np.random.randint(len(far))]
    return np.exp2(a.ravel()).repeat(32)


def f64(x):
    return np.asarray(x).astype(np.float64)


def striped(idx):
    return np.tile(idx.reshape(-1, 16).T, (8, 1)).astype(np.uint16)


def unstriped(offs):
    return offs[:16].T.reshape(-1).astype(np.int64)


E2M1 = np.array([0.0, 0.5, 1.0, 1.5, 2.0, 3.0, 4.0, 6.0, -0.0, -0.5, -1.0, -1.5, -2.0, -3.0, -4.0, -6.0])


def pack_weight(w, fmt):
    k, n = w.shape
    w = f64(np.asarray(w, np.float32).astype(ml_dtypes.bfloat16)).reshape(k // 32, 32, n)
    amax = np.abs(w).max(1)
    if fmt == "e4m3":
        byte = np.frexp(amax)[1] - 1 + 127 - 7
    else:
        mant, ex = np.frexp(amax / 6.0)
        byte = np.where(mant > 0.5, ex, ex - 1) + 127
    byte = np.clip(np.where(amax > 0, byte, 1), 1, 254)
    scaled = (w * np.exp2(127.0 - byte)[:, None, :]).reshape(k, n).astype(np.float32)
    by_word = np.ascontiguousarray(scaled.reshape(k // 512, 128, 4, n).transpose(0, 1, 3, 2))
    if fmt == "e4m3":
        words = by_word.astype(ml_dtypes.float8_e4m3fn).view(np.uint8)
    else:
        c = by_word.astype(ml_dtypes.float4_e2m1fn).view(np.uint8) & 0xF
        words = (c[..., 0::2] | (c[..., 1::2] << 4)).reshape(k // 512, 128, 2 * n)
    return np.ascontiguousarray(words), np.ascontiguousarray(byte.astype(np.uint8).reshape(k // 512, 16, n))


def unpack_weight(words, scales, fmt):
    g, _, n = scales.shape
    words = np.ascontiguousarray(words).reshape(g, 128, n, -1)
    if fmt == "e4m3":
        vals = words.view(ml_dtypes.float8_e4m3fn).astype(np.float64)
    else:
        nib = np.empty((g, 128, n, 4), np.uint8)
        nib[..., 0::2] = words & 0xF
        nib[..., 1::2] = words >> 4
        vals = E2M1[nib]
    vals = vals * np.repeat(np.exp2(scales.astype(np.float64) - 127.0), 8, axis=1)[..., None]
    return vals.transpose(0, 1, 3, 2).reshape(g * 512, n)


def gelu(v):
    return 0.5 * v * (1.0 + np.tanh(np.sqrt(2.0 / np.pi) * (v + 0.044715 * v**3)))


K, T, S, H, T3, S2, P = 1536, 4096, 1024, 512, 2048, 1024, 512


def setup_inputs():
    n = np.random.standard_normal
    s = mx_kscale(K)[:, None]
    u = mx_kscale(H)[:, None]
    tab_words, tab_scales = pack_weight(n((K, T)) * s, "e4m3")
    tab2_words, tab2_scales = pack_weight(n((H, T3)) / np.sqrt(H) / u, "e4m3")
    w4_words, w4_scales = pack_weight(n((K, H)) / np.sqrt(K) / s, "e2m1")
    return {
        "tab_words": tab_words, "tab_scales": tab_scales,
        "offs": striped(np.random.permutation(T)[:S]),
        "w1": (n((K, H)) / np.sqrt(K) / s).astype(np.float32),
        "b1": (0.7 * n(H)).astype(np.float32),
        "w4_words": w4_words, "w4_scales": w4_scales,
        "gain": (np.exp(0.3 * n(H)) * u[:, 0]).astype(np.float32),
        "tab2_words": tab2_words, "tab2_scales": tab2_scales,
        "offs2": striped(np.random.permutation(T3)[:S2]),
        "pos1": striped(np.random.permutation(S)[:P]),
        "pos2": striped(np.random.permutation(S)[:P]),
        "limit": n((S2, P)).astype(np.float32),
    }


def reference(tab_words, tab_scales, offs, w1, b1, w4_words, w4_scales, gain,
              tab2_words, tab2_scales, offs2, pos1, pos2, limit):
    v = unpack_weight(tab_words, tab_scales, "e4m3")[:, unstriped(offs)]
    v2 = unpack_weight(tab2_words, tab2_scales, "e4m3")[:, unstriped(offs2)]
    w4 = unpack_weight(w4_words, w4_scales, "e2m1")
    taste = (mxq(f64(w1), 0, "e4m3").T @ v) + f64(b1)[:, None]
    aroma = w4.T @ v
    h = f64(gain)[:, None] * np.maximum(taste, aroma)
    x1 = np.abs(h[:, unstriped(pos1)])
    x2 = h[:, unstriped(pos2)]
    e1 = v2.T @ mxq(x1, 0, "e4m3")
    e2 = v2.T @ mxq(x2, 0, "e4m3")
    return np.minimum(e1, f64(limit)) + e2

from contextlib import ExitStack

import concourse.mybir as mybir

F32 = mybir.dt.float32
BF16 = mybir.dt.bfloat16
I32 = mybir.dt.int32
U32 = mybir.dt.uint32
U16 = mybir.dt.uint16
U8 = mybir.dt.uint8
FP8X4 = mybir.dt.float8_e4m3fn_x4
FP4X4 = mybir.dt.float4_e2m1fn_x4
ALU = mybir.AluOpType
ACT = mybir.ActivationFunctionType

K, T, S, H, T3, S2, NP = 1536, 4096, 1024, 512, 2048, 1024, 512
P = 128
PASSES = K // 512
NB = 512
HALVES = S // NB
FLOPS = 2 * 2 * K * H * S + 2 * 2 * H * S2 * NP


def tile_list_cheese_chutney_scores_kernel(
    tc, tab_words, tab_scales, offs, w1, b1, w4_words, w4_scales, gain,
    tab2_words, tab2_scales, offs2, pos1, pos2, limit, out,
):
    nc = tc.nc
    with ExitStack() as ctx:
        sb = ctx.enter_context(tc.tile_pool(name="sb", bufs=1))
        arena = ctx.enter_context(tc.tile_pool(name="arena", bufs=1))
        psum = ctx.enter_context(tc.psum_pool(name="psum", bufs=1))

        def tile(name, shape, dtype, tag=None):
            return sb.tile(shape, dtype, name=name, tag=tag or name, align_bytes=64)

        def placed(name, shape, dtype, kib):
            return arena.tile(shape, dtype, name=name, offset=int(kib * 1024), align_bytes=64)

        def bank(name, i):
            return psum.tile([P, NB], F32, name=name, tag="bank%d" % i)

        ts_win = placed("ts_win", [P, T], U8, 42)
        w4s_raw = placed("w4s_raw", [P, PASSES, H], U8, 1)
        t2s_win = placed("t2s_win", [P, T3], U8, 38)
        v_planes = [None] + [tile("v_plane%d" % a, [P, S], U8) for a in range(1, PASSES)]
        nc.vector.memset(ts_win[:].bitcast(I32), 0)
        nc.vector.memset(w4s_raw[:].bitcast(I32), 0)
        nc.vector.memset(t2s_win[:].bitcast(I32), 0)
        for a in range(1, PASSES):
            nc.vector.memset(v_planes[a][96:128, :].bitcast(I32), 0)

        offs_t = sb.tile([P, S // 16], U16, name="offs_t")
        offs2_t = sb.tile([P, S2 // 16], U16, name="offs2_t")
        pos1_t = sb.tile([P, NP // 16], U16, name="pos1_t")
        pos2_t = sb.tile([P, NP // 16], U16, name="pos2_t")
        nc.sync.dma_start(offs_t[:], offs)
        w4_raw = placed("w4_raw", [P, PASSES, 2 * H], U8, 22)
        nc.sync.dma_start(w4_raw[:].bitcast(I32), w4_words.rearrange("a p c -> p a c").bitcast(I32))

        def load_words(a, kib):
            win = placed("tw_win%d" % a, [P, T], U32, kib)
            nc.sync.dma_start(win[:].bitcast(I32), tab_words[a].rearrange("p t i -> p (t i)").bitcast(I32))
            return win

        def load_w1(a, c0, c1, kib):
            raw = placed("w1_raw%d_%d" % (a, c0), [P, 4, c1 - c0], F32, kib)
            nc.sync.dma_start(raw[:], w1[512 * a : 512 * (a + 1), c0:c1].rearrange("(p j) c -> p j c", j=4))
            return (c0, c1, raw)

        tw_win0 = load_words(0, 4)
        nc.sync.dma_start(offs2_t[:], offs2)
        nc.sync.dma_start(pos1_t[:], pos1)
        nc.sync.dma_start(pos2_t[:], pos2)

        for q in range(4):
            queue = nc.scalar if q < 2 else nc.gpsimd
            queue.dma_start(
                ts_win[32 * q : 32 * q + 4 * PASSES, :].bitcast(I32),
                tab_scales[:, 4 * q : 4 * q + 4, :].bitcast(I32),
            )
        for q in range(4):
            nc.gpsimd.dma_start(
                w4s_raw[32 * q : 32 * q + 4, :, :].bitcast(I32),
                w4_scales[:, 4 * q : 4 * q + 4, :].rearrange("a r c -> r a c").bitcast(I32),
            )
        for q in range(4):
            nc.gpsimd.dma_start(
                t2s_win[32 * q + 12 : 32 * q + 16, :].bitcast(I32),
                tab2_scales[0, 4 * q : 4 * q + 4, :].bitcast(I32),
            )
        b1_t = tile("b1_t", [P, 4], F32)
        gain_t = tile("gain_t", [P, 4], F32)
        nc.gpsimd.dma_start(b1_t[:], b1.rearrange("(p t) -> p t", t=4))
        nc.gpsimd.dma_start(gain_t[:], gain.rearrange("(p t) -> p t", t=4))

        w4_codes = tile("w4_codes", [P, PASSES, 2 * H], U8)
        nc.vector.tensor_copy(
            w4_codes[:].bitcast(U16).rearrange("p a (t b i) -> p a b t i", t=4, i=8),
            w4_raw[:].bitcast(U16).rearrange("p a (b i t) -> p a b t i", t=4, i=8),
        )

        tw_win1 = load_words(1, 22)

        v_planes[0] = tile("v_plane0", [P, S], U8)
        nc.vector.tensor_copy(v_planes[0][:], ts_win[:].indirect(offs_t[:]))
        tw_win2 = load_words(2, 44)
        for a in range(1, PASSES):
            nc.scalar.dma_start(
                v_planes[a][0:100, :].bitcast(I32),
                v_planes[0][4 * a : 4 * a + 100, :].bitcast(I32),
            )

        v_codes = [placed("v_codes%d" % a, [P, S], U32, kib) for a, kib in enumerate((40, 2, 36))]
        nc.vector.tensor_copy(v_codes[0][:], tw_win0[:].indirect(offs_t[:]))
        w1_parts = [[load_w1(0, 0, H, 6)], [load_w1(1, 0, H, 14)]]
        w4_planes = tile("w4_planes", [P, PASSES, H], U8)
        nc.vector.tensor_copy(
            w4_planes[:].rearrange("p a (t b i) -> p a b t i", t=4, i=16),
            w4s_raw[:].rearrange("p a (b i t) -> p a b t i", t=4, i=16),
        )
        nc.vector.tensor_copy(v_codes[1][:], tw_win1[:].indirect(offs_t[:]))
        w1_parts.append([load_w1(2, 0, H // 2, 22), load_w1(2, H // 2, H, 26)])
        v2_plane = tile("v2_plane", [P, S2], U8)
        nc.vector.tensor_copy(v2_plane[:], t2s_win[:].indirect(offs2_t[:]))
        for u in range(HALVES):
            nc.vector.tensor_copy(
                v_codes[2][:, NB * u : NB * (u + 1)],
                tw_win2[:].indirect(offs_t[:, 32 * u : 32 * (u + 1)]),
            )
        t2w_win = placed("t2w_win", [P, T3], U32, 44)
        nc.sync.dma_start(t2w_win[:].bitcast(I32), tab2_words[0].rearrange("p t i -> p (t i)").bitcast(I32))
        lim = placed("lim", [P, S2 // P, NP], F32, 56)
        for g in range(2):
            nc.sync.dma_start(
                lim[:, 4 * g : 4 * g + 4, :],
                limit[512 * g : 512 * (g + 1), :].rearrange("(i p) n -> p i n", p=P),
            )

        aroma_ps = [[bank("aroma_ps%d%d" % (t, u), 2 * t + u) for u in range(HALVES)] for t in range(4)]
        for a in range(PASSES):
            for u in range(HALVES):
                for t in range(4):
                    nc.tensor.matmul_mx(
                        aroma_ps[t][u][:],
                        lhsT=w4_codes[:, a, 256 * t : 256 * (t + 1)].bitcast(FP4X4),
                        lhsT_scale=w4_planes[:, a, 128 * t : 128 * (t + 1)],
                        rhs=v_codes[a][:, NB * u : NB * (u + 1)].bitcast(FP8X4),
                        rhs_scale=v_planes[a][:, NB * u : NB * (u + 1)],
                        start=(a == 0),
                        stop=(a == PASSES - 1),
                    )
        best = [tile("best%d" % g, [P, 2, S], F32) for g in range(2)]
        for u in range(HALVES):
            for t in range(4):
                nc.scalar.copy(best[t // 2][:, t % 2, NB * u : NB * (u + 1)], aroma_ps[t][u][:])

        w1_codes, w1_planes = [], []
        for a in range(PASSES):
            w1_bf = placed("w1_bf%d" % a, [P, 4, P, 4], BF16, (52, 72, 76)[a])
            for c0, c1, raw in w1_parts[a]:
                nc.vector.tensor_copy(
                    w1_bf[:, :, c0 // 4 : c1 // 4, :].rearrange("p t m j -> p m t j"),
                    raw[:].rearrange("p j (m t) -> p m t j", t=4),
                )
            codes = tile("w1_codes%d" % a, [P, H], U32)
            plane = tile("w1_plane%d" % a, [P, H], U8)
            step = 4 if a < PASSES - 1 else 2
            for t0 in range(0, 4, step):
                cols = slice(P * t0, P * (t0 + step))
                nc.vector.quantize_mx(
                    codes[:, cols].bitcast(FP8X4),
                    plane[:, cols],
                    w1_bf[:, t0 : t0 + step, :, :].rearrange("p t m j -> p (t m j)"),
                )
            w1_codes.append(codes)
            w1_planes.append(plane)

        h = [tile("h%d" % t, [P, S], F32) for t in range(4)]
        pick1 = tile("pick1", [P, 4, NP], F32)

        def make_h(t):
            for u in range(HALVES):
                cols = slice(NB * u, NB * (u + 1))
                ps = bank("taste_ps%d%d" % (t, u), 2 * t + u)
                for a in range(PASSES):
                    nc.tensor.matmul_mx(
                        ps[:],
                        lhsT=w1_codes[a][:, 128 * t : 128 * (t + 1)].bitcast(FP8X4),
                        lhsT_scale=w1_planes[a][:, 128 * t : 128 * (t + 1)],
                        rhs=v_codes[a][:, cols].bitcast(FP8X4),
                        rhs_scale=v_planes[a][:, cols],
                        start=(a == 0),
                        stop=(a == PASSES - 1),
                    )
                side = best[t // 2][:, t % 2, cols]
                nc.vector.scalar_tensor_tensor(side, ps[:], b1_t[:, t : t + 1], side, ALU.add, ALU.max)
                nc.scalar.activation(h[t][:, cols], side, ACT.Copy, scale=gain_t[:, t : t + 1])

        make_h(0)
        for t in range(4):
            if t + 1 < 4:
                make_h(t + 1)
            nc.vector.tensor_copy(pick1[:, t, :], h[t][:].indirect(pos1_t[:]))

        v2_codes = tile("v2_codes", [P, S2], U32, tag="best0")
        nc.vector.tensor_copy(v2_codes[:], t2w_win[:].indirect(offs2_t[:]))

        def weave(xb, pick, func):
            nc.scalar.activation(
                xb.rearrange("p (c i) t -> p c t i", i=4),
                pick[:].rearrange("p t (c i) -> p c t i", i=4),
                func,
            )

        def quantise(name, xb):
            codes = tile(name + "_codes", [P, NP], U32)
            plane = tile(name + "_plane", [P, NP], U8)
            nc.vector.quantize_mx(codes[:].bitcast(FP8X4), plane[:], xb[:].rearrange("p n t -> p (n t)"))
            return codes, plane

        def score(name, i, codes, plane):
            ps = bank(name, i)
            nc.tensor.matmul_mx(
                ps[:],
                lhsT=v2_codes[:, P * i : P * (i + 1)].bitcast(FP8X4),
                lhsT_scale=v2_plane[12:128, P * i : P * (i + 1)],
                rhs=codes[:].bitcast(FP8X4),
                rhs_scale=plane[:],
                start=True,
                stop=True,
            )
            return ps

        x1_bf = tile("x1_bf", [P, NP, 4], BF16)
        x2_bf = tile("x2_bf", [P, NP, 4], BF16)
        weave(x1_bf[:], pick1, ACT.Abs)

        def pick_hard(u, tag):
            pick2 = tile("pick2_%d" % u, [P, 4, NP // 2], F32, tag=tag)
            for t in range(4):
                nc.vector.tensor_copy(pick2[:, t, :], h[t][:].indirect(pos2_t[:, 16 * u : 16 * (u + 1)]))
            weave(x2_bf[:, 256 * u : 256 * (u + 1), :], pick2, ACT.Copy)

        pick_hard(0, "best1")
        x1_codes, x1_plane = quantise("x1", x1_bf)
        pick_hard(1, "x1_bf")
        x2_codes, x2_plane = quantise("x2", x2_bf)

        for i in range(S2 // P):
            e1 = score("e1_%d" % i, i, x1_codes, x1_plane)
            res = lim[:, i, :]
            nc.vector.tensor_tensor(res, e1[:], res, ALU.min)
        for i in range(S2 // P):
            e2 = score("e2_%d" % i, i, x2_codes, x2_plane)
            res = lim[:, i, :]
            nc.vector.tensor_tensor(res, e2[:], res, ALU.add)
            nc.sync.dma_start(out[P * i : P * (i + 1), :], res)
